import numpy as np
import ml_dtypes


def mxq(x, axis, fmt="e4m3"):
    dtype, down = {"e4m3": (ml_dtypes.float8_e4m3fn, 7), "e5m2": (ml_dtypes.float8_e5m2, 14)}[fmt]
    v = np.moveaxis(np.asarray(x, np.float32).astype(ml_dtypes.bfloat16).astype(np.float64), axis, -1)
    blocks = v.reshape(v.shape[:-1] + (-1, 32))
    amax = np.abs(blocks).max(-1, keepdims=True)
    byte = np.maximum(np.where(amax > 0, np.frexp(amax)[1] - 1 + 127, 0) - down, 1)
    scale = np.exp2(byte - 127.0)
    codes = (blocks / scale).astype(np.float32).astype(dtype).astype(np.float64)
    return np.moveaxis((codes * scale).reshape(v.shape), -1, axis)


WIDE = False


def mx_kscale(k):
    if not WIDE:
        return np.ones(k)
    levels = np.array([10, -10, 5, -5, 0])
    if k % 512:
        return np.exp2(np.random.permutation(np.resize(levels, k // 32))).repeat(32)
    a = np.empty((k // 512, 16))
    for p in range(k // 512):
        a[p, :8] = np.random.permutation(np.resize(levels, 8))
        for g in range(8):
            far = levels[np.abs(levels - a[p, g]) >= 10]
            a[p, g + 8] = far[np.random.randint(len(far))]
    return np.exp2(a.ravel()).repeat(32)


def f64(x):
    return np.asarray(x).astype(np.float64)


def striped(idx):
    return np.tile(idx.reshape(-1, 16).T, (8, 1)).astype(np.uint16)


def unstriped(offs):
    return offs[:16].T.reshape(-1).astype(np.int64)


def striped8(idx):
    return np.concatenate([x.reshape(-1, 16).T for x in idx]).astype(np.uint16)


def runs(offs, k):
    lists = np.stack([offs[16 * r : 16 * r + 16].T.reshape(-1) for r in range(8)]).astype(np.int64)
    return lists[np.arange(k) % 512 // 64]


def pack_weight(w):
    k, n = w.shape
    w = f64(np.asarray(w, np.float32).astype(ml_dtypes.bfloat16)).reshape(k // 32, 32, n)
    amax = np.abs(w).max(1)
    byte = np.clip(np.where(amax > 0, np.frexp(amax)[1] - 1 + 127 - 7, 1), 1, 254)
    scaled = (w * np.exp2(127.0 - byte)[:, None, :]).reshape(k, n).astype(np.float32)
    words = np.ascontiguousarray(scaled.reshape(k // 512, 128, 4, n).transpose(0, 1, 3, 2)).astype(ml_dtypes.float8_e4m3fn).view(np.uint8)
    return words, np.ascontiguousarray(byte.astype(np.uint8).reshape(k // 512, 16, n))


def unpack_weight(words, scales):
    g, p, n, _ = words.shape
    vals = np.ascontiguousarray(words).view(ml_dtypes.float8_e4m3fn).astype(np.float64) * np.repeat(np.exp2(scales.astype(np.float64) - 127.0), 8, axis=1)[..., None]
    return vals.transpose(0, 1, 3, 2).reshape(g * 512, n)


K, T, S, N, H = 512, 2048, 512, 512, 512


def setup_inputs():
    n = np.random.standard_normal
    s = mx_kscale(K)[:, None]
    u = mx_kscale(H)
    packed_xT = pack_weight(n((K, T)) * s)
    return {
        "x_words": packed_xT[0],
        "x_scales": packed_xT[1],
        "w1": (n((K, H)) / np.sqrt(K) / s).astype(np.float32),
        "tau": np.random.uniform(0.3, 0.9, (H, 1)).astype(np.float32),
        "gn": (np.random.uniform(0.5, 1.5, (H, 1)) * u[:, None]).astype(np.float32),
        "w2": (n((H, N)) / np.sqrt(2 * H) / u[:, None]).astype(np.float32),
        "w3": (n((K, N)) / np.sqrt(2 * K) / s).astype(np.float32),
        "offs": striped(np.random.permutation(T)[:S]),
        "n1": striped8(np.stack([np.random.permutation(S) for _ in range(8)])),
        "n2": striped8(np.stack([np.random.permutation(S) for _ in range(8)])),
        "hz": striped8(np.random.randint(0, T, (8, S))),
        "n3": striped8(np.stack([np.random.permutation(S) for _ in range(8)])),
        "n4": striped8(np.stack([np.random.permutation(S) for _ in range(8)])),
    }


def reference(x_words, x_scales, w1, tau, gn, w2, w3, offs, n1, n2, hz, n3, n4):
    xq = unpack_weight(x_words, x_scales)[:, unstriped(offs)]
    y = mxq(f64(w1), 0, "e4m3").T @ xq
    low = y.min(axis=1, keepdims=True)
    ea = np.exp(f64(tau) * (low - (y[np.arange(H)[:, None], runs(n1, H)])))
    z = f64(gn) * (y - (2.0 * (ea * (y[np.arange(H)[:, None], runs(n2, H)]))))
    x_hz = unpack_weight(x_words, x_scales)[np.arange(K)[:, None], runs(hz, K)]
    h = mxq(f64(w2), 0, "e4m3").T @ mxq(z, 0, "e4m3") + mxq(f64(w3), 0, "e4m3").T @ x_hz
    pa = h[np.arange(N)[:, None], runs(n3, N)]
    kr = np.exp(-0.5 * ((h - pa) ** 2))
    pb = h[np.arange(N)[:, None], runs(n4, N)]
    kr2 = np.exp(-0.5 * ((h - pb) ** 2))
    return (kr * pa + kr2 * pb) / (kr + kr2 + 0.5)

@@ -1,0 +1,302 @@
+from contextlib import ExitStack
+
+import concourse.mybir as mybir
+
+K, T, S, N, H = 512, 2048, 512, 512, 512
+FLOPS = 3 * 2 * 512 * 512 * 512
+
+F32 = mybir.dt.float32
+BF16 = mybir.dt.bfloat16
+I32 = mybir.dt.int32
+U32 = mybir.dt.uint32
+U16 = mybir.dt.uint16
+U8 = mybir.dt.uint8
+FP8X4 = mybir.dt.float8_e4m3fn_x4
+ACT = mybir.ActivationFunctionType
+ALU = mybir.AluOpType
+
+P = 128
+PACK = 4
+HALF = S // 2
+LIST_COLS = S // 16
+
+
+def tile_picked_mixhebzkern_none_p_kernel(
+    tc, x_words, x_scales, w1, tau, gn, w2, w3, offs, n1, n2, hz, n3, n4, out
+):
+    nc = tc.nc
+    with ExitStack() as ctx:
+        lists = ctx.enter_context(tc.tile_pool(name="lists", bufs=1))
+        keep = ctx.enter_context(tc.tile_pool(name="keep", bufs=1))
+        ring = ctx.enter_context(tc.tile_pool(name="ring", bufs=2))
+        psum = ctx.enter_context(tc.psum_pool(name="psum", bufs=1))
+
+        def load_list(src, name):
+            tile = lists.tile([P, LIST_COLS], U16, name=name)
+            nc.sync.dma_start(tile[:], src)
+            return tile
+
+        def half_of(tile, half):
+            return tile[:, half * (LIST_COLS // 2) : (half + 1) * (LIST_COLS // 2)]
+
+        scale_rows = x_scales[0].bitcast(I32)
+
+        xs = keep.tile([P, T], U8, name="xs", align_bytes=64)
+        hz_scales = keep.tile([P, S], U8, name="hz_scales", align_bytes=64)
+        nc.vector.memset(xs[:, 0:1280].bitcast(I32), 0)
+        nc.gpsimd.memset(xs[:, 1280:T].bitcast(I32), 0)
+        nc.gpsimd.memset(hz_scales[:].bitcast(I32), 0)
+
+        offs_t = load_list(offs, "offs_t")
+        hz_t = load_list(hz, "hz_t")
+        for q in range(4):
+            nc.sync.dma_start(xs[32 * q : 32 * q + 4, :].bitcast(I32), scale_rows[4 * q : 4 * q + 4, :])
+        nc.sync.dma_start(xs[4:P:8, :].bitcast(I32), scale_rows)
+        xw = keep.tile([P, T], I32, name="xw", align_bytes=64)
+        nc.sync.dma_start(xw[:], x_words[0].rearrange("p n t -> p (n t)").bitcast(I32))
+        w1_rows = w1.rearrange("(p j) c -> p j c", j=PACK)
+        w1_raw = []
+        for a in range(2):
+            raw = keep.tile([P, PACK, H // 2], F32, name=f"w1_raw{a}")
+            nc.sync.dma_start(raw[:], w1_rows[:, :, a * (H // 2) : (a + 1) * (H // 2)])
+            w1_raw.append(raw)
+        tau_t = keep.tile([P, PACK], F32, name="tau_t")
+        gn_t = keep.tile([P, PACK], F32, name="gn_t")
+        nc.gpsimd.dma_start(tau_t[:], tau.rearrange("(p t) o -> p (t o)", t=PACK))
+        nc.gpsimd.dma_start(gn_t[:], gn.rearrange("(p t) o -> p (t o)", t=PACK))
+        n2_t = load_list(n2, "n2_t")
+        n1_t = load_list(n1, "n1_t")
+        w2_raw = keep.tile([P, PACK, N], F32, name="w2_raw")
+        w3_raw = keep.tile([P, PACK, N], F32, name="w3_raw")
+        nc.sync.dma_start(w2_raw[:], w2.rearrange("(p j) c -> p j c", j=PACK))
+        nc.sync.dma_start(w3_raw[:], w3.rearrange("(p j) c -> p j c", j=PACK))
+        n3_t = load_list(n3, "n3_t")
+        n4_t = load_list(n4, "n4_t")
+
+        pick_scales = keep.tile([P, S], U8, name="pick_scales", align_bytes=64)
+        pick_words = keep.tile([P, S], U32, name="pick_words", align_bytes=64)
+        hz_bytes = keep.tile([P, S], U8, name="hz_bytes", align_bytes=64)
+        nc.vector.tensor_copy(pick_scales[:], xs[:].indirect(offs_t[:]))
+        nc.vector.tensor_copy(hz_bytes[:], xs[:].indirect(hz_t[:]))
+        nc.vector.tensor_copy(pick_words[:], xw[:].bitcast(U32).indirect(offs_t[:]))
+        hz_words = keep.tile([P, S], U32, name="hz_words", align_bytes=64)
+        nc.vector.tensor_copy(hz_words[:], xw[:].bitcast(U32).indirect(hz_t[:]))
+        neg_tau = keep.tile([P, PACK], F32, name="neg_tau")
+        gn_m2 = keep.tile([P, PACK], F32, name="gn_m2")
+        nc.gpsimd.tensor_scalar(neg_tau[:], tau_t[:], -1.0, 0.0, ALU.mult, ALU.add)
+        nc.gpsimd.tensor_scalar(gn_m2[:], gn_t[:], -2.0, 0.0, ALU.mult, ALU.add)
+
+        w1_codes = keep.tile([P, PACK, P], U32, name="w1_codes", align_bytes=64)
+        w1_scales = keep.tile([P, PACK, P], U8, name="w1_scales", align_bytes=64)
+        M2 = P // 2
+
+        def deal(engine_copy, raw, t0, t1, name):
+            m = raw.shape[2] // PACK
+            dealt = keep.tile([P, t1 - t0, m, PACK], BF16, name=name, align_bytes=64)
+            engine_copy(
+                dealt[:].rearrange("p t m j -> p m j t"),
+                raw[:].rearrange("p j (m t) -> p m j t", t=PACK)[:, :, :, t0:t1],
+            )
+            return dealt
+
+        first = deal(nc.scalar.copy, w1_raw[0], 0, 4, "w1_dealt0")
+        second = [
+            deal(nc.vector.tensor_copy, w1_raw[1], 0, 2, "w1_dealt1"),
+            deal(nc.scalar.copy, w1_raw[1], 2, 4, "w1_dealt2"),
+        ]
+        y_ps = []
+        for t in range(PACK):
+            nc.vector.quantize_mx(
+                out=w1_codes[:, t, 0:M2].bitcast(FP8X4),
+                scales=w1_scales[:, t, 0:M2],
+                in_=first[:, t].rearrange("p m j -> p (m j)"),
+            )
+            nc.vector.quantize_mx(
+                out=w1_codes[:, t, M2:P].bitcast(FP8X4),
+                scales=w1_scales[:, t, M2:P],
+                in_=second[t // 2][:, t % 2].rearrange("p m j -> p (m j)"),
+            )
+            bank = psum.tile([P, S], F32, name=f"y_ps{t}")
+            nc.tensor.matmul_mx(
+                out=bank[:],
+                lhsT=w1_codes[:, t, :].bitcast(FP8X4),
+                lhsT_scale=w1_scales[:, t, :],
+                rhs=pick_words[:].bitcast(FP8X4),
+                rhs_scale=pick_scales[:],
+                start=True,
+                stop=True,
+            )
+            y_ps.append(bank)
+
+        y_sb, lows = [], []
+        for t in range(PACK):
+            y_t = keep.tile([P, S], F32, name=f"y{t}")
+            low = keep.tile([P, 1], F32, name=f"low{t}", tag=f"low{t}", align_bytes=64)
+            nc.vector.tensor_scalar(y_t[:], y_ps[t][:], 1.0, None, ALU.mult, ALU.min, accum_out=low[:])
+            y_sb.append(y_t)
+            lows.append(low)
+
+        for j in range(4):
+            nc.sync.dma_start(hz_scales[j:P:32, :].bitcast(I32), hz_bytes[4 + 8 * j : P : 32, :].bitcast(I32))
+
+        def quantize_pair(dealt, name):
+            codes = keep.tile([P, 2, P], U32, name=name + "_codes", align_bytes=64)
+            scales = keep.tile([P, 2, P], U8, name=name + "_scales", align_bytes=64)
+            nc.vector.quantize_mx(
+                out=codes[:].rearrange("p t m -> p (t m)").bitcast(FP8X4),
+                scales=scales[:].rearrange("p t m -> p (t m)"),
+                in_=dealt[:].rearrange("p t m j -> p (t m j)"),
+            )
+            return codes, scales
+
+        bias = [keep.tile([P, 1], F32, name=f"bias{t}") for t in range(PACK)]
+        z = [keep.tile([P, PACK, HALF], F32, name=f"z{half}") for half in range(2)]
+
+        def fetch_y(t, half):
+            y2 = ring.tile([P, HALF], F32, name="y2", bufs=4)
+            ea = ring.tile([P, HALF], F32, name="ea", bufs=4)
+            nc.scalar.activation(y2[:], y_sb[t][:].indirect(half_of(n2_t, half)), ACT.Copy)
+            if half == 0:
+                nc.scalar.activation(bias[t][:], lows[t][:], ACT.Copy, scale=tau_t[:, t : t + 1])
+            nc.scalar.activation(
+                ea[:], y_sb[t][:].indirect(half_of(n1_t, half)), ACT.Exp,
+                bias=bias[t][:], scale=neg_tau[:, t : t + 1],
+            )
+            return y2, ea
+
+        def make_z(t, half, y2, ea):
+            cols = slice(half * HALF, (half + 1) * HALF)
+            u = ring.tile([P, HALF], F32, name="u", bufs=4)
+            nc.vector.scalar_tensor_tensor(u[:], ea[:], gn_m2[:, t : t + 1], y2[:], ALU.mult, ALU.mult)
+            nc.vector.scalar_tensor_tensor(
+                z[half][:, t, :], y_ps[t][:, cols], gn_t[:, t : t + 1], u[:], ALU.mult, ALU.add
+            )
+
+        def weave_z(half):
+            woven = keep.tile([P, HALF, PACK], BF16, name=f"z_woven{half}", align_bytes=64)
+            nc.vector.tensor_copy(
+                woven[:].rearrange("p (c i) t -> p c t i", i=4), z[half][:].rearrange("p t (c i) -> p c t i", i=4)
+            )
+            return woven
+
+        def quantize_z(half, woven):
+            codes = keep.tile([P, HALF], U32, name=f"z_codes{half}", align_bytes=64)
+            scales = keep.tile([P, HALF], U8, name=f"z_scales{half}", align_bytes=64)
+            nc.vector.quantize_mx(
+                out=codes[:].bitcast(FP8X4), scales=scales[:], in_=woven[:].rearrange("p c t -> p (c t)")
+            )
+            return codes, scales
+
+        dealt_pairs, w_mx, z_mx = [], [], []
+        pairs = [(w2_raw, 0, "w2a"), (w2_raw, 2, "w2b"), (w3_raw, 0, "w3a"), (w3_raw, 2, "w3b")]
+        for t in range(PACK):
+            fetched = fetch_y(t, 0)
+            raw, t0, name = pairs[t]
+            dealt_pairs.append(deal(nc.vector.tensor_copy, raw, t0, t0 + 2, name + "_dealt"))
+            if t >= 1:
+                w_mx.append(quantize_pair(dealt_pairs[t - 1], pairs[t - 1][2]))
+            make_z(t, 0, *fetched)
+        for t in range(PACK):
+            fetched = fetch_y(t, 1)
+            if t == 0:
+                woven = weave_z(0)
+                w_mx.append(quantize_pair(dealt_pairs[PACK - 1], pairs[PACK - 1][2]))
+                z_mx.append(quantize_z(0, woven))
+            make_z(t, 1, *fetched)
+        z_mx.append(quantize_z(1, weave_z(1)))
+        w2_mx, w3_mx = w_mx[0:2], w_mx[2:4]
+
+        h_ps = [psum.tile([P, S], F32, name=f"h_ps{t}") for t in range(PACK)]
+        for t in range(PACK):
+            nc.tensor.matmul_mx(
+                out=h_ps[t][:],
+                lhsT=w3_mx[t // 2][0][:, t % 2, :].bitcast(FP8X4),
+                lhsT_scale=w3_mx[t // 2][1][:, t % 2, :],
+                rhs=hz_words[:].bitcast(FP8X4),
+                rhs_scale=hz_scales[:],
+                start=True,
+                stop=False,
+            )
+        for half in range(2):
+            for t in range(PACK):
+                nc.tensor.matmul_mx(
+                    out=h_ps[t][:, half * HALF : (half + 1) * HALF],
+                    lhsT=w2_mx[t // 2][0][:, t % 2, :].bitcast(FP8X4),
+                    lhsT_scale=w2_mx[t // 2][1][:, t % 2, :],
+                    rhs=z_mx[half][0][:].bitcast(FP8X4),
+                    rhs_scale=z_mx[half][1][:],
+                    start=False,
+                    stop=(half == 1),
+                )
+
+        num = keep.tile([P, PACK, S], F32, name="num")
+        den_sq = keep.tile([P, PACK, S], F32, name="den_sq")
+        h_sb = [keep.tile([P, S], F32, name=f"h{t}") for t in range(PACK)]
+        picked = [keep.tile([P, 2, S], F32, name=f"picked{t}") for t in range(PACK)]
+        diff = [keep.tile([P, 2, S], F32, name=f"diff{t}") for t in range(PACK)]
+        kern = [keep.tile([P, 2, S], F32, name=f"kern{t}") for t in range(PACK)]
+        den = [keep.tile([P, S], F32, name=f"den{t}") for t in range(PACK)]
+
+        def fetch_b(t):
+            for half in range(2):
+                cols = slice(half * HALF, (half + 1) * HALF)
+                nc.scalar.activation(picked[t][:, 1, cols], h_sb[t][:].indirect(half_of(n4_t, half)), ACT.Copy)
+
+        def fetch_a(t):
+            for half in range(2):
+                cols = slice(half * HALF, (half + 1) * HALF)
+                nc.vector.tensor_copy(picked[t][:, 0, cols], h_sb[t][:].indirect(half_of(n3_t, half)))
+            for e in range(2):
+                nc.vector.tensor_tensor(diff[t][:, e, :], picked[t][:, e, :], h_ps[t][:], ALU.subtract)
+
+        def weights(t, cols):
+            width = cols.stop - cols.start
+            sq = ring.tile([P, 2, width], F32, name="sq")
+            nc.scalar.activation(sq[:], diff[t][:, :, cols], ACT.Square)
+            nc.scalar.activation(kern[t][:, :, cols], sq[:], ACT.Exp, scale=-0.5)
+
+        def sums(t, cols, last):
+            width = cols.stop - cols.start
+            prod = ring.tile([P, 2, width], F32, name="prod")
+            nc.vector.scalar_tensor_tensor(
+                den[t][:, cols], kern[t][:, 0, cols], 0.5, kern[t][:, 1, cols], ALU.add, ALU.add
+            )
+            nc.vector.tensor_tensor(prod[:], kern[t][:, :, cols], picked[t][:, :, cols], ALU.mult)
+            if last:
+                nc.vector.tensor_tensor(den_sq[:, t, cols], den[t][:, cols], den[t][:, cols], ALU.mult)
+            nc.vector.tensor_tensor(num[:, t, cols], prod[:, 0, :], prod[:, 1, :], ALU.add)
+
+        def square_den(t):
+            nc.scalar.activation(den_sq[:, t, :], den[t][:], ACT.Square)
+
+        whole = slice(0, S)
+        nc.vector.tensor_copy(h_sb[0][:], h_ps[0][:])
+        nc.scalar.copy(h_sb[1][:], h_ps[1][:])
+        fetch_b(0)
+        fetch_a(0)
+        fetch_b(1)
+        for t in range(PACK - 1):
+            fetch_a(t + 1)
+            weights(t, whole)
+            if t + 2 < PACK:
+                nc.scalar.copy(h_sb[t + 2][:], h_ps[t + 2][:])
+                fetch_b(t + 2)
+            sums(t, whole, False)
+            if t >= 1:
+                square_den(t - 1)
+        for half in range(2):
+            cols = slice(half * HALF, (half + 1) * HALF)
+            weights(PACK - 1, cols)
+            if half == 0:
+                square_den(PACK - 2)
+            sums(PACK - 1, cols, True)
+
+        out_rows = out.rearrange("(p t) c -> p t c", t=PACK)
+        QUART = S // 4
+        for part in range(4):
+            cols = slice(part * QUART, (part + 1) * QUART)
+            res = keep.tile([P, PACK, QUART], F32, name=f"res{part}")
+            inv = ring.tile([P, PACK, QUART], F32, name="inv", bufs=4)
+            nc.scalar.activation(inv[:], den_sq[:, :, cols], ACT.Abs_reciprocal_sqrt)
+            nc.vector.tensor_tensor(res[:], num[:, :, cols], inv[:], ALU.mult)
+            nc.sync.dma_start(out_rows[:, :, cols], res[:])

@@ -1,6 +1,7 @@
 from contextlib import ExitStack
 
 import concourse.mybir as mybir
+from concourse.masks import make_identity
 
 K, T, S, N, H = 512, 2048, 512, 512, 512
 FLOPS = 3 * 2 * 512 * 512 * 512
@@ -47,6 +48,11 @@ def tile_picked_mixhebzkern_none_p_kernel(
         nc.gpsimd.memset(xs[:, 1280:T].bitcast(I32), 0)
         nc.gpsimd.memset(hz_scales[:].bitcast(I32), 0)
 
+        ident = keep.tile([P, P], F32, name="ident")
+        make_identity(nc, ident[:])
+        half_const = keep.tile([P, 1], F32, name="half_const")
+        nc.gpsimd.memset(half_const[:], 0.5)
+
         offs_t = load_list(offs, "offs_t")
         hz_t = load_list(hz, "hz_t")
         for q in range(4):
@@ -62,10 +68,10 @@ def tile_picked_mixhebzkern_none_p_kernel(
             w1_raw.append(raw)
         tau_t = keep.tile([P, PACK], F32, name="tau_t")
         gn_t = keep.tile([P, PACK], F32, name="gn_t")
-        nc.gpsimd.dma_start(tau_t[:], tau.rearrange("(p t) o -> p (t o)", t=PACK))
-        nc.gpsimd.dma_start(gn_t[:], gn.rearrange("(p t) o -> p (t o)", t=PACK))
         n2_t = load_list(n2, "n2_t")
         n1_t = load_list(n1, "n1_t")
+        nc.sync.dma_start(tau_t[:], tau.rearrange("(p t) o -> p (t o)", t=PACK))
+        nc.sync.dma_start(gn_t[:], gn.rearrange("(p t) o -> p (t o)", t=PACK))
         w2_raw = keep.tile([P, PACK, N], F32, name="w2_raw")
         w3_raw = keep.tile([P, PACK, N], F32, name="w3_raw")
         nc.sync.dma_start(w2_raw[:], w2.rearrange("(p j) c -> p j c", j=PACK))
@@ -83,8 +89,6 @@ def tile_picked_mixhebzkern_none_p_kernel(
         nc.vector.tensor_copy(hz_words[:], xw[:].bitcast(U32).indirect(hz_t[:]))
         neg_tau = keep.tile([P, PACK], F32, name="neg_tau")
         gn_m2 = keep.tile([P, PACK], F32, name="gn_m2")
-        nc.gpsimd.tensor_scalar(neg_tau[:], tau_t[:], -1.0, 0.0, ALU.mult, ALU.add)
-        nc.gpsimd.tensor_scalar(gn_m2[:], gn_t[:], -2.0, 0.0, ALU.mult, ALU.add)
 
         w1_codes = keep.tile([P, PACK, P], U32, name="w1_codes", align_bytes=64)
         w1_scales = keep.tile([P, PACK, P], U8, name="w1_scales", align_bytes=64)
@@ -116,7 +120,7 @@ def tile_picked_mixhebzkern_none_p_kernel(
                 scales=w1_scales[:, t, M2:P],
                 in_=second[t // 2][:, t % 2].rearrange("p m j -> p (m j)"),
             )
-            bank = psum.tile([P, S], F32, name=f"y_ps{t}")
+            bank = psum.tile([P, S], F32, name=f"y_ps{t}", tag=f"bank{t}")
             nc.tensor.matmul_mx(
                 out=bank[:],
                 lhsT=w1_codes[:, t, :].bitcast(FP8X4),
@@ -128,6 +132,8 @@ def tile_picked_mixhebzkern_none_p_kernel(
             )
             y_ps.append(bank)
 
+        nc.scalar.activation(neg_tau[:], tau_t[:], ACT.Copy, scale=-1.0)
+        nc.scalar.activation(gn_m2[:], gn_t[:], ACT.Copy, scale=-2.0)
         y_sb, lows = [], []
         for t in range(PACK):
             y_t = keep.tile([P, S], F32, name=f"y{t}")
@@ -169,7 +175,7 @@ def tile_picked_mixhebzkern_none_p_kernel(
             u = ring.tile([P, HALF], F32, name="u", bufs=4)
             nc.vector.scalar_tensor_tensor(u[:], ea[:], gn_m2[:, t : t + 1], y2[:], ALU.mult, ALU.mult)
             nc.vector.scalar_tensor_tensor(
-                z[half][:, t, :], y_ps[t][:, cols], gn_t[:, t : t + 1], u[:], ALU.mult, ALU.add
+                z[half][:, t, :], y_sb[t][:, cols], gn_t[:, t : t + 1], u[:], ALU.mult, ALU.add
             )
 
         def weave_z(half):
@@ -206,54 +212,72 @@ def tile_picked_mixhebzkern_none_p_kernel(
         z_mx.append(quantize_z(1, weave_z(1)))
         w2_mx, w3_mx = w_mx[0:2], w_mx[2:4]
 
-        h_ps = [psum.tile([P, S], F32, name=f"h_ps{t}") for t in range(PACK)]
-        for t in range(PACK):
-            nc.tensor.matmul_mx(
-                out=h_ps[t][:],
-                lhsT=w3_mx[t // 2][0][:, t % 2, :].bitcast(FP8X4),
-                lhsT_scale=w3_mx[t // 2][1][:, t % 2, :],
-                rhs=hz_words[:].bitcast(FP8X4),
-                rhs_scale=hz_scales[:],
-                start=True,
-                stop=False,
-            )
+        ORDER = (2, 0, 1, 3)
+        h_sb = [keep.tile([P, S], F32, name=f"h{t}") for t in range(PACK)]
+        h_ps = {}
         for half in range(2):
-            for t in range(PACK):
+            cols = slice(half * HALF, (half + 1) * HALF)
+            for t in ORDER:
+                h_ps[t, half] = psum.tile([P, HALF], F32, name=f"h_ps{t}_{half}", tag=f"bank{PACK * (1 - half) + t}")
                 nc.tensor.matmul_mx(
-                    out=h_ps[t][:, half * HALF : (half + 1) * HALF],
+                    out=h_ps[t, half][:],
+                    lhsT=w3_mx[t // 2][0][:, t % 2, :].bitcast(FP8X4),
+                    lhsT_scale=w3_mx[t // 2][1][:, t % 2, :],
+                    rhs=hz_words[:, cols].bitcast(FP8X4),
+                    rhs_scale=hz_scales[:, cols],
+                    start=True,
+                    stop=False,
+                )
+        for half in range(2):
+            for t in ORDER:
+                nc.tensor.matmul_mx(
+                    out=h_ps[t, half][:],
                     lhsT=w2_mx[t // 2][0][:, t % 2, :].bitcast(FP8X4),
                     lhsT_scale=w2_mx[t // 2][1][:, t % 2, :],
                     rhs=z_mx[half][0][:].bitcast(FP8X4),
                     rhs_scale=z_mx[half][1][:],
                     start=False,
-                    stop=(half == 1),
+                    stop=True,
                 )
+        for t in ORDER:
+            nc.scalar.copy(h_sb[t][:, 0:HALF], h_ps[t, 0][:])
 
-        num = keep.tile([P, PACK, S], F32, name="num")
+        TURNED = 2
+        num = keep.tile([P, PACK - TURNED, S], F32, name="num")
         den_sq = keep.tile([P, PACK, S], F32, name="den_sq")
-        h_sb = [keep.tile([P, S], F32, name=f"h{t}") for t in range(PACK)]
         picked = [keep.tile([P, 2, S], F32, name=f"picked{t}") for t in range(PACK)]
-        diff = [keep.tile([P, 2, S], F32, name=f"diff{t}") for t in range(PACK)]
-        kern = [keep.tile([P, 2, S], F32, name=f"kern{t}") for t in range(PACK)]
-        den = [keep.tile([P, S], F32, name=f"den{t}") for t in range(PACK)]
+        diff = {t: keep.tile([P, 2, S], F32, name=f"diff{t}") for t in range(TURNED, PACK)}
+        kern = {t: keep.tile([P, 2, S], F32, name=f"kern{t}") for t in range(TURNED, PACK)}
+        den = {t: keep.tile([P, S], F32, name=f"den{t}") for t in range(TURNED, PACK)}
+        halves = [slice(0, HALF), slice(HALF, S)]
 
-        def fetch_b(t):
-            for half in range(2):
-                cols = slice(half * HALF, (half + 1) * HALF)
-                nc.scalar.activation(picked[t][:, 1, cols], h_sb[t][:].indirect(half_of(n4_t, half)), ACT.Copy)
+        def fetch_b(t, half, sign):
+            nc.scalar.activation(
+                picked[t][:, 1, halves[half]], h_sb[t][:].indirect(half_of(n4_t, half)), ACT.Copy, scale=sign
+            )
 
-        def fetch_a(t):
-            for half in range(2):
-                cols = slice(half * HALF, (half + 1) * HALF)
-                nc.vector.tensor_copy(picked[t][:, 0, cols], h_sb[t][:].indirect(half_of(n3_t, half)))
+        def fetch_a(t, half):
+            nc.vector.tensor_copy(picked[t][:, 0, halves[half]], h_sb[t][:].indirect(half_of(n3_t, half)))
+
+        def fetch_neg_a(t, half):
+            nc.vector.tensor_scalar(
+                picked[t][:, 0, halves[half]], h_sb[t][:].indirect(half_of(n3_t, half)), -1.0, 0.0, ALU.mult, ALU.add
+            )
+
+        def subtract(t):
             for e in range(2):
-                nc.vector.tensor_tensor(diff[t][:, e, :], picked[t][:, e, :], h_ps[t][:], ALU.subtract)
+                nc.vector.tensor_tensor(diff[t][:, e, :], picked[t][:, e, :], h_sb[t][:], ALU.subtract)
 
-        def weights(t, cols):
+        def weights(t, cols, tag):
             width = cols.stop - cols.start
-            sq = ring.tile([P, 2, width], F32, name="sq")
+            sq = ring.tile([P, 2, width], F32, name="sq", tag=tag, bufs=1)
             nc.scalar.activation(sq[:], diff[t][:, :, cols], ACT.Square)
             nc.scalar.activation(kern[t][:, :, cols], sq[:], ACT.Exp, scale=-0.5)
+
+        def square_on_vector(t):
+            sq = ring.tile([P, 2, S], F32, name="sq_first", bufs=1)
+            nc.vector.tensor_tensor(sq[:], diff[t][:], diff[t][:], ALU.mult)
+            return sq
 
         def sums(t, cols, last):
             width = cols.stop - cols.start
@@ -264,39 +288,110 @@ def tile_picked_mixhebzkern_none_p_kernel(
             nc.vector.tensor_tensor(prod[:], kern[t][:, :, cols], picked[t][:, :, cols], ALU.mult)
             if last:
                 nc.vector.tensor_tensor(den_sq[:, t, cols], den[t][:, cols], den[t][:, cols], ALU.mult)
-            nc.vector.tensor_tensor(num[:, t, cols], prod[:, 0, :], prod[:, 1, :], ALU.add)
+            nc.vector.tensor_tensor(num[:, t - TURNED, cols], prod[:, 0, :], prod[:, 1, :], ALU.add)
 
-        def square_den(t):
-            nc.scalar.activation(den_sq[:, t, :], den[t][:], ACT.Square)
+        def add_turned(dst, first, second):
+            nc.tensor.matmul(dst, first, ident[:], start=True, stop=False, is_transpose=True)
+            nc.tensor.matmul(dst, second, ident[:], start=False, stop=True, is_transpose=True)
+
+        def turn_diff(t, half):
+            diff_ps = psum.tile([P, 2, 2, P], F32, name="diff_ps", tag=f"bank{half}")
+            for e in range(2):
+                for b in range(2):
+                    cols = slice(half * HALF + b * P, half * HALF + (b + 1) * P)
+                    add_turned(diff_ps[:, e, b, :], h_sb[t][:, cols], picked[t][:, e, cols])
+            return diff_ps
+
+        def turn_vals(t, half):
+            vals_ps = psum.tile([P, 2, 2, P], F32, name="vals_ps", tag=f"bank{2 + half}")
+            for e in range(2):
+                for b in range(2):
+                    cols = slice(half * HALF + b * P, half * HALF + (b + 1) * P)
+                    nc.tensor.transpose(vals_ps[:, e, b, :], picked[t][:, e, cols], ident[:])
+            return vals_ps
+
+        def turn(t, half):
+            return turn_diff(t, half), turn_vals(t, half)
+
+        def turned_weights(diff_ps):
+            sq = ring.tile([P, 2, 2, P], F32, name="sq_turned")
+            k_turned = ring.tile([P, 2, 2, P], F32, name="k_turned", bufs=4)
+            nc.scalar.activation(sq[:], diff_ps[:], ACT.Square)
+            nc.scalar.activation(k_turned[:], sq[:], ACT.Exp, scale=-0.5)
+            return k_turned
+
+        def turn_back(half, k_turned, vals_ps, num_ps, sum_ps):
+            prod = ring.tile([P, 2, 2, P], F32, name="prod_turned", bufs=4)
+            nc.vector.tensor_tensor(prod[:], k_turned[:], vals_ps[:], ALU.mult)
+            for b in range(2):
+                cols = slice(half * HALF + b * P, half * HALF + (b + 1) * P)
+                add_turned(sum_ps[:, cols], k_turned[:, 0, b, :], k_turned[:, 1, b, :])
+            for b in range(2):
+                cols = slice(half * HALF + b * P, half * HALF + (b + 1) * P)
+                add_turned(num_ps[:, cols], prod[:, 0, b, :], prod[:, 1, b, :])
 
         whole = slice(0, S)
-        nc.vector.tensor_copy(h_sb[0][:], h_ps[0][:])
-        nc.scalar.copy(h_sb[1][:], h_ps[1][:])
-        fetch_b(0)
-        fetch_a(0)
-        fetch_b(1)
-        for t in range(PACK - 1):
-            fetch_a(t + 1)
-            weights(t, whole)
-            if t + 2 < PACK:
-                nc.scalar.copy(h_sb[t + 2][:], h_ps[t + 2][:])
-                fetch_b(t + 2)
-            sums(t, whole, False)
-            if t >= 1:
-                square_den(t - 1)
+        num_ps, sum_ps, steps = {}, {}, {}
+
+        def open_sums(t):
+            num_ps[t] = psum.tile([P, S], F32, name=f"num_ps{t}", tag=f"bank{PACK + t}")
+            sum_ps[t] = psum.tile([P, S], F32, name=f"sum_ps{t}", tag=f"bank{PACK + 2 + t}")
+
+        def square_sum(t):
+            nc.scalar.activation(den_sq[:, t, :], sum_ps[t][:], ACT.Square, bias=half_const[:])
+
+        nc.vector.tensor_copy(h_sb[2][:, HALF:S], h_ps[2, 1][:])
+        nc.scalar.copy(h_sb[0][:, HALF:S], h_ps[0, 1][:])
         for half in range(2):
-            cols = slice(half * HALF, (half + 1) * HALF)
-            weights(PACK - 1, cols)
+            fetch_a(2, half)
+            fetch_b(2, half, 1.0)
+        for half in range(2):
+            fetch_neg_a(0, half)
+            fetch_b(0, half, -1.0)
+        diffs0 = [turn_diff(0, half) for half in range(2)]
+        vals0 = [turn_vals(0, half) for half in range(2)]
+        subtract(2)
+        nc.vector.tensor_copy(h_sb[1][:, HALF:S], h_ps[1, 1][:])
+        sq_first = square_on_vector(2)
+        for half in range(2):
+            fetch_b(1, half, -1.0)
+        k0 = [turned_weights(diffs0[0])]
+        nc.scalar.activation(kern[2][:], sq_first[:], ACT.Exp, scale=-0.5)
+        for half in range(2):
+            fetch_neg_a(1, half)
+        nc.vector.tensor_copy(h_sb[3][:, HALF:S], h_ps[3, 1][:])
+        k0.append(turned_weights(diffs0[1]))
+        diffs1 = [turn_diff(1, half) for half in range(2)]
+        open_sums(0)
+        vals1 = []
+        for half in range(2):
+            turn_back(half, k0[half], vals0[half], num_ps[0], sum_ps[0])
+            vals1.append(turn_vals(1, half))
+            fetch_b(3, half, 1.0)
             if half == 0:
-                square_den(PACK - 2)
-            sums(PACK - 1, cols, True)
+                sums(2, halves[0], True)
+        for half in range(2):
+            fetch_a(3, half)
+        k1 = [turned_weights(diffs1[half]) for half in range(2)]
+        subtract(3)
+        open_sums(1)
+        for half in range(2):
+            turn_back(half, k1[half], vals1[half], num_ps[1], sum_ps[1])
+        sums(2, halves[1], True)
+        for half in range(2):
+            sq = ring.tile([P, 2, HALF], F32, name="sq", tag=f"sq_last{half}", bufs=1)
+            nc.scalar.activation(sq[:], diff[3][:, :, halves[half]], ACT.Square)
+            square_sum(half)
+            nc.scalar.activation(kern[3][:, :, halves[half]], sq[:], ACT.Exp, scale=-0.5)
+            sums(3, halves[half], True)
 
         out_rows = out.rearrange("(p t) c -> p t c", t=PACK)
-        QUART = S // 4
-        for part in range(4):
-            cols = slice(part * QUART, (part + 1) * QUART)
-            res = keep.tile([P, PACK, QUART], F32, name=f"res{part}")
-            inv = ring.tile([P, PACK, QUART], F32, name="inv", bufs=4)
-            nc.scalar.activation(inv[:], den_sq[:, :, cols], ACT.Abs_reciprocal_sqrt)
-            nc.vector.tensor_tensor(res[:], num[:, :, cols], inv[:], ALU.mult)
-            nc.sync.dma_start(out_rows[:, :, cols], res[:])
+        inv = ring.tile([P, PACK, S], F32, name="inv", tag="sq_last1", bufs=1)
+        for t, cols in [(2, whole), (0, whole), (1, whole), (3, halves[0]), (3, halves[1])]:
+            res = ring.tile([P, cols.stop - cols.start], F32, name="res", bufs=5)
+            nc.scalar.activation(inv[:, t, cols], den_sq[:, t, cols], ACT.Abs_reciprocal_sqrt)
+            if t < TURNED:
+                nc.vector.scalar_tensor_tensor(res[:], num_ps[t][:, cols], -1.0, inv[:, t, cols], ALU.mult, ALU.mult)
+            else:
+                nc.vector.tensor_tensor(res[:], num[:, t - TURNED, cols], inv[:, t, cols], ALU.mult)
+            nc.sync.dma_start(out_rows[:, t, cols], res[:])

@@ -264,9 +264,9 @@ def tile_picked_mixhebzkern_none_p_kernel(
                 picked[t][:, 0, halves[half]], h_sb[t][:].indirect(half_of(n3_t, half)), -1.0, 0.0, ALU.mult, ALU.add
             )
 
-        def subtract(t):
+        def subtract(t, engine):
             for e in range(2):
-                nc.vector.tensor_tensor(diff[t][:, e, :], picked[t][:, e, :], h_sb[t][:], ALU.subtract)
+                engine.tensor_tensor(diff[t][:, e, :], picked[t][:, e, :], h_sb[t][:], ALU.subtract)
 
         def weights(t, cols, tag):
             width = cols.stop - cols.start
@@ -276,7 +276,8 @@ def tile_picked_mixhebzkern_none_p_kernel(
 
         def square_on_vector(t):
             sq = ring.tile([P, 2, S], F32, name="sq_first", bufs=1)
-            nc.vector.tensor_tensor(sq[:], diff[t][:], diff[t][:], ALU.mult)
+            for e in range(2):
+                nc.gpsimd.tensor_tensor(sq[:, e, :], diff[t][:, e, :], diff[t][:, e, :], ALU.mult)
             return sq
 
         def sums(t, cols, last):
@@ -295,7 +296,7 @@ def tile_picked_mixhebzkern_none_p_kernel(
             nc.tensor.matmul(dst, second, ident[:], start=False, stop=True, is_transpose=True)
 
         def turn_diff(t, half):
-            diff_ps = psum.tile([P, 2, 2, P], F32, name="diff_ps", tag=f"bank{half}")
+            diff_ps = psum.tile([P, 2, 2, P], F32, name="diff_ps", tag=f"bank{6 * t + half}")
             for e in range(2):
                 for b in range(2):
                     cols = slice(half * HALF + b * P, half * HALF + (b + 1) * P)
@@ -313,11 +314,10 @@ def tile_picked_mixhebzkern_none_p_kernel(
         def turn(t, half):
             return turn_diff(t, half), turn_vals(t, half)
 
-        def turned_weights(diff_ps):
-            sq = ring.tile([P, 2, 2, P], F32, name="sq_turned")
+        def turned_weights(diff_ps, sq):
             k_turned = ring.tile([P, 2, 2, P], F32, name="k_turned", bufs=4)
-            nc.scalar.activation(sq[:], diff_ps[:], ACT.Square)
-            nc.scalar.activation(k_turned[:], sq[:], ACT.Exp, scale=-0.5)
+            nc.scalar.activation(sq, diff_ps[:], ACT.Square)
+            nc.scalar.activation(k_turned[:], sq, ACT.Exp, scale=-0.5)
             return k_turned
 
         def turn_back(half, k_turned, vals_ps, num_ps, sum_ps):
@@ -335,7 +335,7 @@ def tile_picked_mixhebzkern_none_p_kernel(
 
         def open_sums(t):
             num_ps[t] = psum.tile([P, S], F32, name=f"num_ps{t}", tag=f"bank{PACK + t}")
-            sum_ps[t] = psum.tile([P, S], F32, name=f"sum_ps{t}", tag=f"bank{PACK + 2 + t}")
+            sum_ps[t] = psum.tile([P, S], F32, name=f"sum_ps{t}", tag=f"bank{t}")
 
         def square_sum(t):
             nc.scalar.activation(den_sq[:, t, :], sum_ps[t][:], ACT.Square, bias=half_const[:])
@@ -345,49 +345,48 @@ def tile_picked_mixhebzkern_none_p_kernel(
         for half in range(2):
             fetch_a(2, half)
             fetch_b(2, half, 1.0)
+        subtract(2, nc.gpsimd)
+        sq_first = square_on_vector(2)
         for half in range(2):
             fetch_neg_a(0, half)
             fetch_b(0, half, -1.0)
+        for t in (1, 3):
+            nc.vector.tensor_copy(h_sb[t][:, HALF:S], h_ps[t, 1][:])
         diffs0 = [turn_diff(0, half) for half in range(2)]
         vals0 = [turn_vals(0, half) for half in range(2)]
-        subtract(2)
-        nc.vector.tensor_copy(h_sb[1][:, HALF:S], h_ps[1, 1][:])
-        sq_first = square_on_vector(2)
-        for half in range(2):
-            fetch_b(1, half, -1.0)
-        k0 = [turned_weights(diffs0[0])]
-        nc.scalar.activation(kern[2][:], sq_first[:], ACT.Exp, scale=-0.5)
         for half in range(2):
             fetch_neg_a(1, half)
-        nc.vector.tensor_copy(h_sb[3][:, HALF:S], h_ps[3, 1][:])
-        k0.append(turned_weights(diffs0[1]))
+            fetch_b(1, half, -1.0)
         diffs1 = [turn_diff(1, half) for half in range(2)]
+        for half in range(2):
+            fetch_a(3, half)
+            fetch_b(3, half, 1.0)
+        subtract(3, nc.vector)
+        sq_last = ring.tile([P, 2, S], F32, name="sq_last", bufs=1)
+        nc.vector.tensor_tensor(sq_last[:], diff[3][:], diff[3][:], ALU.mult)
+        sq0 = ring.tile([P, 2, 2, 2, P], F32, name="sq_turned", bufs=1)
+        k0 = [turned_weights(diffs0[half], sq0[:, half]) for half in range(2)]
+        nc.scalar.activation(kern[2][:], sq_first[:], ACT.Exp, scale=-0.5)
+        nc.scalar.activation(kern[3][:], sq_last[:], ACT.Exp, scale=-0.5)
         open_sums(0)
         vals1 = []
         for half in range(2):
             turn_back(half, k0[half], vals0[half], num_ps[0], sum_ps[0])
             vals1.append(turn_vals(1, half))
-            fetch_b(3, half, 1.0)
-            if half == 0:
-                sums(2, halves[0], True)
-        for half in range(2):
-            fetch_a(3, half)
-        k1 = [turned_weights(diffs1[half]) for half in range(2)]
-        subtract(3)
+        sums(2, whole, True)
+        square_sum(0)
+        sq1 = ring.tile([P, 2, 2, 2, P], F32, name="sq1", tag="sq_last", bufs=1)
+        k1 = [turned_weights(diffs1[half], sq1[:, half]) for half in range(2)]
+        sums(3, whole, True)
         open_sums(1)
         for half in range(2):
             turn_back(half, k1[half], vals1[half], num_ps[1], sum_ps[1])
-        sums(2, halves[1], True)
-        for half in range(2):
-            sq = ring.tile([P, 2, HALF], F32, name="sq", tag=f"sq_last{half}", bufs=1)
-            nc.scalar.activation(sq[:], diff[3][:, :, halves[half]], ACT.Square)
-            square_sum(half)
-            nc.scalar.activation(kern[3][:, :, halves[half]], sq[:], ACT.Exp, scale=-0.5)
-            sums(3, halves[half], True)
 
         out_rows = out.rearrange("(p t) c -> p t c", t=PACK)
-        inv = ring.tile([P, PACK, S], F32, name="inv", tag="sq_last1", bufs=1)
-        for t, cols in [(2, whole), (0, whole), (1, whole), (3, halves[0]), (3, halves[1])]:
+        inv = ring.tile([P, PACK, S], F32, name="inv", tag="sq_last", bufs=1)
+        for t, cols in [(2, whole), (0, whole), (3, whole), (1, halves[0]), (1, halves[1])]:
+            if (t, cols) == (3, whole):
+                square_sum(1)
             res = ring.tile([P, cols.stop - cols.start], F32, name="res", bufs=5)
             nc.scalar.activation(inv[:, t, cols], den_sq[:, t, cols], ACT.Abs_reciprocal_sqrt)
             if t < TURNED:

@@ -4,7 +4,7 @@ import concourse.mybir as mybir
 from concourse.masks import make_identity
 
 K, T, S, N, H = 512, 2048, 512, 512, 512
-FLOPS = 3 * 2 * 512 * 512 * 512
+FLOPS = 2 * S * (K * H + H * N + K * N)
 
 F32 = mybir.dt.float32
 BF16 = mybir.dt.bfloat16
@@ -20,6 +20,11 @@ P = 128
 PACK = 4
 HALF = S // 2
 LIST_COLS = S // 16
+QUADRANT = 32
+VECTOR_CLEARS = 1280
+TURNED = 2
+H_BANK = (0, 6, 2, 4)
+FETCH_DEPTH = 4
 
 
 def tile_picked_mixhebzkern_none_p_kernel(
@@ -32,6 +37,9 @@ def tile_picked_mixhebzkern_none_p_kernel(
         ring = ctx.enter_context(tc.tile_pool(name="ring", bufs=2))
         psum = ctx.enter_context(tc.psum_pool(name="psum", bufs=1))
 
+        halves = [slice(0, HALF), slice(HALF, S)]
+        whole = slice(0, S)
+
         def load_list(src, name):
             tile = lists.tile([P, LIST_COLS], U16, name=name)
             nc.sync.dma_start(tile[:], src)
@@ -41,11 +49,10 @@ def tile_picked_mixhebzkern_none_p_kernel(
             return tile[:, half * (LIST_COLS // 2) : (half + 1) * (LIST_COLS // 2)]
 
         scale_rows = x_scales[0].bitcast(I32)
-
         xs = keep.tile([P, T], U8, name="xs", align_bytes=64)
         hz_scales = keep.tile([P, S], U8, name="hz_scales", align_bytes=64)
-        nc.vector.memset(xs[:, 0:1280].bitcast(I32), 0)
-        nc.gpsimd.memset(xs[:, 1280:T].bitcast(I32), 0)
+        nc.vector.memset(xs[:, 0:VECTOR_CLEARS].bitcast(I32), 0)
+        nc.gpsimd.memset(xs[:, VECTOR_CLEARS:T].bitcast(I32), 0)
         nc.gpsimd.memset(hz_scales[:].bitcast(I32), 0)
 
         ident = keep.tile([P, P], F32, name="ident")
@@ -56,15 +63,17 @@ def tile_picked_mixhebzkern_none_p_kernel(
         offs_t = load_list(offs, "offs_t")
         hz_t = load_list(hz, "hz_t")
         for q in range(4):
-            nc.sync.dma_start(xs[32 * q : 32 * q + 4, :].bitcast(I32), scale_rows[4 * q : 4 * q + 4, :])
+            nc.sync.dma_start(
+                xs[QUADRANT * q : QUADRANT * q + 4, :].bitcast(I32), scale_rows[4 * q : 4 * q + 4, :]
+            )
         nc.sync.dma_start(xs[4:P:8, :].bitcast(I32), scale_rows)
         xw = keep.tile([P, T], I32, name="xw", align_bytes=64)
         nc.sync.dma_start(xw[:], x_words[0].rearrange("p n t -> p (n t)").bitcast(I32))
         w1_rows = w1.rearrange("(p j) c -> p j c", j=PACK)
         w1_raw = []
-        for a in range(2):
-            raw = keep.tile([P, PACK, H // 2], F32, name=f"w1_raw{a}")
-            nc.sync.dma_start(raw[:], w1_rows[:, :, a * (H // 2) : (a + 1) * (H // 2)])
+        for part in range(2):
+            raw = keep.tile([P, PACK, H // 2], F32, name=f"w1_raw{part}")
+            nc.sync.dma_start(raw[:], w1_rows[:, :, part * (H // 2) : (part + 1) * (H // 2)])
             w1_raw.append(raw)
         tau_t = keep.tile([P, PACK], F32, name="tau_t")
         gn_t = keep.tile([P, PACK], F32, name="gn_t")
@@ -90,10 +99,6 @@ def tile_picked_mixhebzkern_none_p_kernel(
         neg_tau = keep.tile([P, PACK], F32, name="neg_tau")
         gn_m2 = keep.tile([P, PACK], F32, name="gn_m2")
 
-        w1_codes = keep.tile([P, PACK, P], U32, name="w1_codes", align_bytes=64)
-        w1_scales = keep.tile([P, PACK, P], U8, name="w1_scales", align_bytes=64)
-        M2 = P // 2
-
         def deal(engine_copy, raw, t0, t1, name):
             m = raw.shape[2] // PACK
             dealt = keep.tile([P, t1 - t0, m, PACK], BF16, name=name, align_bytes=64)
@@ -103,23 +108,22 @@ def tile_picked_mixhebzkern_none_p_kernel(
             )
             return dealt
 
-        first = deal(nc.scalar.copy, w1_raw[0], 0, 4, "w1_dealt0")
-        second = [
+        w1_codes = keep.tile([P, PACK, P], U32, name="w1_codes", align_bytes=64)
+        w1_scales = keep.tile([P, PACK, P], U8, name="w1_scales", align_bytes=64)
+        w1_low = deal(nc.scalar.copy, w1_raw[0], 0, 4, "w1_dealt0")
+        w1_high = [
             deal(nc.vector.tensor_copy, w1_raw[1], 0, 2, "w1_dealt1"),
             deal(nc.scalar.copy, w1_raw[1], 2, 4, "w1_dealt2"),
         ]
         y_ps = []
         for t in range(PACK):
-            nc.vector.quantize_mx(
-                out=w1_codes[:, t, 0:M2].bitcast(FP8X4),
-                scales=w1_scales[:, t, 0:M2],
-                in_=first[:, t].rearrange("p m j -> p (m j)"),
-            )
-            nc.vector.quantize_mx(
-                out=w1_codes[:, t, M2:P].bitcast(FP8X4),
-                scales=w1_scales[:, t, M2:P],
-                in_=second[t // 2][:, t % 2].rearrange("p m j -> p (m j)"),
-            )
+            for part, dealt in enumerate((w1_low[:, t], w1_high[t // 2][:, t % 2])):
+                m_cols = slice(part * (P // 2), (part + 1) * (P // 2))
+                nc.vector.quantize_mx(
+                    out=w1_codes[:, t, m_cols].bitcast(FP8X4),
+                    scales=w1_scales[:, t, m_cols],
+                    in_=dealt.rearrange("p m j -> p (m j)"),
+                )
             bank = psum.tile([P, S], F32, name=f"y_ps{t}", tag=f"bank{t}")
             nc.tensor.matmul_mx(
                 out=bank[:],
@@ -137,13 +141,18 @@ def tile_picked_mixhebzkern_none_p_kernel(
         y_sb, lows = [], []
         for t in range(PACK):
             y_t = keep.tile([P, S], F32, name=f"y{t}")
-            low = keep.tile([P, 1], F32, name=f"low{t}", tag=f"low{t}", align_bytes=64)
+            low = keep.tile([P, 1], F32, name=f"low{t}", align_bytes=64)
             nc.vector.tensor_scalar(y_t[:], y_ps[t][:], 1.0, None, ALU.mult, ALU.min, accum_out=low[:])
             y_sb.append(y_t)
             lows.append(low)
 
         for j in range(4):
-            nc.sync.dma_start(hz_scales[j:P:32, :].bitcast(I32), hz_bytes[4 + 8 * j : P : 32, :].bitcast(I32))
+            nc.sync.dma_start(
+                hz_scales[j:P:QUADRANT, :].bitcast(I32), hz_bytes[4 + 8 * j : P : QUADRANT, :].bitcast(I32)
+            )
+
+        bias = [keep.tile([P, 1], F32, name=f"bias{t}") for t in range(PACK)]
+        z = [keep.tile([P, PACK, HALF], F32, name=f"z{half}") for half in range(2)]
 
         def quantize_pair(dealt, name):
             codes = keep.tile([P, 2, P], U32, name=name + "_codes", align_bytes=64)
@@ -155,27 +164,26 @@ def tile_picked_mixhebzkern_none_p_kernel(
             )
             return codes, scales
 
-        bias = [keep.tile([P, 1], F32, name=f"bias{t}") for t in range(PACK)]
-        z = [keep.tile([P, PACK, HALF], F32, name=f"z{half}") for half in range(2)]
-
         def fetch_y(t, half):
-            y2 = ring.tile([P, HALF], F32, name="y2", bufs=4)
-            ea = ring.tile([P, HALF], F32, name="ea", bufs=4)
-            nc.scalar.activation(y2[:], y_sb[t][:].indirect(half_of(n2_t, half)), ACT.Copy)
+            y_n2 = ring.tile([P, HALF], F32, name="y_n2", bufs=FETCH_DEPTH)
+            ea = ring.tile([P, HALF], F32, name="ea", bufs=FETCH_DEPTH)
+            nc.scalar.activation(y_n2[:], y_sb[t][:].indirect(half_of(n2_t, half)), ACT.Copy)
             if half == 0:
                 nc.scalar.activation(bias[t][:], lows[t][:], ACT.Copy, scale=tau_t[:, t : t + 1])
             nc.scalar.activation(
-                ea[:], y_sb[t][:].indirect(half_of(n1_t, half)), ACT.Exp,
-                bias=bias[t][:], scale=neg_tau[:, t : t + 1],
+                ea[:],
+                y_sb[t][:].indirect(half_of(n1_t, half)),
+                ACT.Exp,
+                bias=bias[t][:],
+                scale=neg_tau[:, t : t + 1],
             )
-            return y2, ea
+            return y_n2, ea
 
-        def make_z(t, half, y2, ea):
-            cols = slice(half * HALF, (half + 1) * HALF)
-            u = ring.tile([P, HALF], F32, name="u", bufs=4)
-            nc.vector.scalar_tensor_tensor(u[:], ea[:], gn_m2[:, t : t + 1], y2[:], ALU.mult, ALU.mult)
+        def make_z(t, half, y_n2, ea):
+            u = ring.tile([P, HALF], F32, name="u", bufs=FETCH_DEPTH)
+            nc.vector.scalar_tensor_tensor(u[:], ea[:], gn_m2[:, t : t + 1], y_n2[:], ALU.mult, ALU.mult)
             nc.vector.scalar_tensor_tensor(
-                z[half][:, t, :], y_sb[t][:, cols], gn_t[:, t : t + 1], u[:], ALU.mult, ALU.add
+                z[half][:, t, :], y_sb[t][:, halves[half]], gn_t[:, t : t + 1], u[:], ALU.mult, ALU.add
             )
 
         def weave_z(half):
@@ -206,30 +214,29 @@ def tile_picked_mixhebzkern_none_p_kernel(
             fetched = fetch_y(t, 1)
             if t == 0:
                 woven = weave_z(0)
-                w_mx.append(quantize_pair(dealt_pairs[PACK - 1], pairs[PACK - 1][2]))
+                w_mx.append(quantize_pair(dealt_pairs[-1], pairs[-1][2]))
                 z_mx.append(quantize_z(0, woven))
             make_z(t, 1, *fetched)
         z_mx.append(quantize_z(1, weave_z(1)))
         w2_mx, w3_mx = w_mx[0:2], w_mx[2:4]
 
-        ORDER = (2, 0, 1, 3)
+        h_order = (2, 0, 1, 3)
         h_sb = [keep.tile([P, S], F32, name=f"h{t}") for t in range(PACK)]
         h_ps = {}
         for half in range(2):
-            cols = slice(half * HALF, (half + 1) * HALF)
-            for t in ORDER:
-                h_ps[t, half] = psum.tile([P, HALF], F32, name=f"h_ps{t}_{half}", tag=f"bank{PACK * (1 - half) + t}")
+            for t in h_order:
+                h_ps[t, half] = psum.tile([P, HALF], F32, name=f"h_ps{t}_{half}", tag=f"bank{H_BANK[t] + half}")
                 nc.tensor.matmul_mx(
                     out=h_ps[t, half][:],
                     lhsT=w3_mx[t // 2][0][:, t % 2, :].bitcast(FP8X4),
                     lhsT_scale=w3_mx[t // 2][1][:, t % 2, :],
-                    rhs=hz_words[:, cols].bitcast(FP8X4),
-                    rhs_scale=hz_scales[:, cols],
+                    rhs=hz_words[:, halves[half]].bitcast(FP8X4),
+                    rhs_scale=hz_scales[:, halves[half]],
                     start=True,
                     stop=False,
                 )
         for half in range(2):
-            for t in ORDER:
+            for t in h_order:
                 nc.tensor.matmul_mx(
                     out=h_ps[t, half][:],
                     lhsT=w2_mx[t // 2][0][:, t % 2, :].bitcast(FP8X4),
@@ -239,158 +246,137 @@ def tile_picked_mixhebzkern_none_p_kernel(
                     start=False,
                     stop=True,
                 )
-        for t in ORDER:
-            nc.scalar.copy(h_sb[t][:, 0:HALF], h_ps[t, 0][:])
+        for t in h_order:
+            nc.scalar.copy(h_sb[t][:, halves[0]], h_ps[t, 0][:])
 
-        TURNED = 2
         num = keep.tile([P, PACK - TURNED, S], F32, name="num")
         den_sq = keep.tile([P, PACK, S], F32, name="den_sq")
         picked = [keep.tile([P, 2, S], F32, name=f"picked{t}") for t in range(PACK)]
         diff = {t: keep.tile([P, 2, S], F32, name=f"diff{t}") for t in range(TURNED, PACK)}
         kern = {t: keep.tile([P, 2, S], F32, name=f"kern{t}") for t in range(TURNED, PACK)}
         den = {t: keep.tile([P, S], F32, name=f"den{t}") for t in range(TURNED, PACK)}
-        halves = [slice(0, HALF), slice(HALF, S)]
+        num_ps, sum_ps = {}, {}
 
-        def fetch_b(t, half, sign):
-            nc.scalar.activation(
-                picked[t][:, 1, halves[half]], h_sb[t][:].indirect(half_of(n4_t, half)), ACT.Copy, scale=sign
-            )
-
-        def fetch_a(t, half):
-            nc.vector.tensor_copy(picked[t][:, 0, halves[half]], h_sb[t][:].indirect(half_of(n3_t, half)))
-
-        def fetch_neg_a(t, half):
-            nc.vector.tensor_scalar(
-                picked[t][:, 0, halves[half]], h_sb[t][:].indirect(half_of(n3_t, half)), -1.0, 0.0, ALU.mult, ALU.add
-            )
+        def fetch_h(t):
+            for half in range(2):
+                by_n3 = h_sb[t][:].indirect(half_of(n3_t, half))
+                by_n4 = h_sb[t][:].indirect(half_of(n4_t, half))
+                if t < TURNED:
+                    nc.vector.tensor_scalar(picked[t][:, 0, halves[half]], by_n3, -1.0, 0.0, ALU.mult, ALU.add)
+                    nc.scalar.activation(picked[t][:, 1, halves[half]], by_n4, ACT.Copy, scale=-1.0)
+                else:
+                    nc.vector.tensor_copy(picked[t][:, 0, halves[half]], by_n3)
+                    nc.scalar.activation(picked[t][:, 1, halves[half]], by_n4, ACT.Copy, scale=1.0)
 
         def subtract(t, engine):
             for e in range(2):
                 engine.tensor_tensor(diff[t][:, e, :], picked[t][:, e, :], h_sb[t][:], ALU.subtract)
 
-        def weights(t, cols, tag):
-            width = cols.stop - cols.start
-            sq = ring.tile([P, 2, width], F32, name="sq", tag=tag, bufs=1)
-            nc.scalar.activation(sq[:], diff[t][:, :, cols], ACT.Square)
-            nc.scalar.activation(kern[t][:, :, cols], sq[:], ACT.Exp, scale=-0.5)
+        def plain_sums(t):
+            prod = ring.tile([P, 2, S], F32, name="prod")
+            nc.vector.scalar_tensor_tensor(den[t][:], kern[t][:, 0, :], 0.5, kern[t][:, 1, :], ALU.add, ALU.add)
+            nc.vector.tensor_tensor(prod[:], kern[t][:], picked[t][:], ALU.mult)
+            nc.vector.tensor_tensor(den_sq[:, t, :], den[t][:], den[t][:], ALU.mult)
+            nc.vector.tensor_tensor(num[:, t - TURNED, :], prod[:, 0, :], prod[:, 1, :], ALU.add)
 
-        def square_on_vector(t):
-            sq = ring.tile([P, 2, S], F32, name="sq_first", bufs=1)
-            for e in range(2):
-                nc.gpsimd.tensor_tensor(sq[:, e, :], diff[t][:, e, :], diff[t][:, e, :], ALU.mult)
-            return sq
+        def block(half, b):
+            return slice(half * HALF + b * P, half * HALF + (b + 1) * P)
 
-        def sums(t, cols, last):
-            width = cols.stop - cols.start
-            prod = ring.tile([P, 2, width], F32, name="prod")
-            nc.vector.scalar_tensor_tensor(
-                den[t][:, cols], kern[t][:, 0, cols], 0.5, kern[t][:, 1, cols], ALU.add, ALU.add
-            )
-            nc.vector.tensor_tensor(prod[:], kern[t][:, :, cols], picked[t][:, :, cols], ALU.mult)
-            if last:
-                nc.vector.tensor_tensor(den_sq[:, t, cols], den[t][:, cols], den[t][:, cols], ALU.mult)
-            nc.vector.tensor_tensor(num[:, t - TURNED, cols], prod[:, 0, :], prod[:, 1, :], ALU.add)
-
-        def add_turned(dst, first, second):
-            nc.tensor.matmul(dst, first, ident[:], start=True, stop=False, is_transpose=True)
-            nc.tensor.matmul(dst, second, ident[:], start=False, stop=True, is_transpose=True)
+        def add_transposed(dst, term0, term1):
+            nc.tensor.matmul(dst, term0, ident[:], start=True, stop=False, is_transpose=True)
+            nc.tensor.matmul(dst, term1, ident[:], start=False, stop=True, is_transpose=True)
 
         def turn_diff(t, half):
             diff_ps = psum.tile([P, 2, 2, P], F32, name="diff_ps", tag=f"bank{6 * t + half}")
             for e in range(2):
                 for b in range(2):
-                    cols = slice(half * HALF + b * P, half * HALF + (b + 1) * P)
-                    add_turned(diff_ps[:, e, b, :], h_sb[t][:, cols], picked[t][:, e, cols])
+                    add_transposed(diff_ps[:, e, b, :], h_sb[t][:, block(half, b)], picked[t][:, e, block(half, b)])
             return diff_ps
 
         def turn_vals(t, half):
             vals_ps = psum.tile([P, 2, 2, P], F32, name="vals_ps", tag=f"bank{2 + half}")
             for e in range(2):
                 for b in range(2):
-                    cols = slice(half * HALF + b * P, half * HALF + (b + 1) * P)
-                    nc.tensor.transpose(vals_ps[:, e, b, :], picked[t][:, e, cols], ident[:])
+                    nc.tensor.transpose(vals_ps[:, e, b, :], picked[t][:, e, block(half, b)], ident[:])
             return vals_ps
 
-        def turn(t, half):
-            return turn_diff(t, half), turn_vals(t, half)
-
         def turned_weights(diff_ps, sq):
-            k_turned = ring.tile([P, 2, 2, P], F32, name="k_turned", bufs=4)
+            k_turned = ring.tile([P, 2, 2, P], F32, name="k_turned", bufs=FETCH_DEPTH)
             nc.scalar.activation(sq, diff_ps[:], ACT.Square)
             nc.scalar.activation(k_turned[:], sq, ACT.Exp, scale=-0.5)
             return k_turned
-
-        def turn_back(half, k_turned, vals_ps, num_ps, sum_ps):
-            prod = ring.tile([P, 2, 2, P], F32, name="prod_turned", bufs=4)
-            nc.vector.tensor_tensor(prod[:], k_turned[:], vals_ps[:], ALU.mult)
-            for b in range(2):
-                cols = slice(half * HALF + b * P, half * HALF + (b + 1) * P)
-                add_turned(sum_ps[:, cols], k_turned[:, 0, b, :], k_turned[:, 1, b, :])
-            for b in range(2):
-                cols = slice(half * HALF + b * P, half * HALF + (b + 1) * P)
-                add_turned(num_ps[:, cols], prod[:, 0, b, :], prod[:, 1, b, :])
-
-        whole = slice(0, S)
-        num_ps, sum_ps, steps = {}, {}, {}
 
         def open_sums(t):
             num_ps[t] = psum.tile([P, S], F32, name=f"num_ps{t}", tag=f"bank{PACK + t}")
             sum_ps[t] = psum.tile([P, S], F32, name=f"sum_ps{t}", tag=f"bank{t}")
 
+        def turn_back(t, half, k_turned, vals_ps):
+            prod_turned = ring.tile([P, 2, 2, P], F32, name="prod_turned", bufs=FETCH_DEPTH)
+            nc.vector.tensor_tensor(prod_turned[:], k_turned[:], vals_ps[:], ALU.mult)
+            for b in range(2):
+                add_transposed(sum_ps[t][:, block(half, b)], k_turned[:, 0, b, :], k_turned[:, 1, b, :])
+            for b in range(2):
+                add_transposed(num_ps[t][:, block(half, b)], prod_turned[:, 0, b, :], prod_turned[:, 1, b, :])
+
         def square_sum(t):
             nc.scalar.activation(den_sq[:, t, :], sum_ps[t][:], ACT.Square, bias=half_const[:])
 
-        nc.vector.tensor_copy(h_sb[2][:, HALF:S], h_ps[2, 1][:])
-        nc.scalar.copy(h_sb[0][:, HALF:S], h_ps[0, 1][:])
-        for half in range(2):
-            fetch_a(2, half)
-            fetch_b(2, half, 1.0)
+        nc.vector.tensor_copy(h_sb[2][:, halves[1]], h_ps[2, 1][:])
+        nc.scalar.copy(h_sb[0][:, halves[1]], h_ps[0, 1][:])
+        fetch_h(2)
         subtract(2, nc.gpsimd)
-        sq_first = square_on_vector(2)
-        for half in range(2):
-            fetch_neg_a(0, half)
-            fetch_b(0, half, -1.0)
+        sq2 = ring.tile([P, 2, S], F32, name="sq2", bufs=1)
+        for e in range(2):
+            nc.gpsimd.tensor_tensor(sq2[:, e, :], diff[2][:, e, :], diff[2][:, e, :], ALU.mult)
+        fetch_h(0)
         for t in (1, 3):
-            nc.vector.tensor_copy(h_sb[t][:, HALF:S], h_ps[t, 1][:])
+            nc.vector.tensor_copy(h_sb[t][:, halves[1]], h_ps[t, 1][:])
         diffs0 = [turn_diff(0, half) for half in range(2)]
         vals0 = [turn_vals(0, half) for half in range(2)]
-        for half in range(2):
-            fetch_neg_a(1, half)
-            fetch_b(1, half, -1.0)
+        fetch_h(1)
         diffs1 = [turn_diff(1, half) for half in range(2)]
-        for half in range(2):
-            fetch_a(3, half)
-            fetch_b(3, half, 1.0)
-        subtract(3, nc.vector)
-        sq_last = ring.tile([P, 2, S], F32, name="sq_last", bufs=1)
-        nc.vector.tensor_tensor(sq_last[:], diff[3][:], diff[3][:], ALU.mult)
-        sq0 = ring.tile([P, 2, 2, 2, P], F32, name="sq_turned", bufs=1)
+        fetch_h(3)
+        for e in range(2):
+            for half in range(2):
+                nc.vector.tensor_tensor(
+                    diff[3][:, e, halves[half]], picked[3][:, e, halves[half]], h_ps[3, half][:], ALU.subtract
+                )
+
+        sq3 = ring.tile([P, 2, S], F32, name="sq3", tag="exp_order", bufs=1)
+        nc.vector.tensor_tensor(sq3[:], diff[3][:], diff[3][:], ALU.mult)
+        sq0 = ring.tile([P, 2, 2, 2, P], F32, name="sq0", bufs=1)
         k0 = [turned_weights(diffs0[half], sq0[:, half]) for half in range(2)]
-        nc.scalar.activation(kern[2][:], sq_first[:], ACT.Exp, scale=-0.5)
-        nc.scalar.activation(kern[3][:], sq_last[:], ACT.Exp, scale=-0.5)
+        nc.scalar.activation(kern[2][:], sq2[:], ACT.Exp, scale=-0.5)
+        nc.scalar.activation(kern[3][:], sq3[:], ACT.Exp, scale=-0.5)
         open_sums(0)
         vals1 = []
         for half in range(2):
-            turn_back(half, k0[half], vals0[half], num_ps[0], sum_ps[0])
+            turn_back(0, half, k0[half], vals0[half])
             vals1.append(turn_vals(1, half))
-        sums(2, whole, True)
+        plain_sums(2)
         square_sum(0)
-        sq1 = ring.tile([P, 2, 2, 2, P], F32, name="sq1", tag="sq_last", bufs=1)
+        sq1 = ring.tile([P, 2, 2, 2, P], F32, name="sq1", tag="exp_order", bufs=1)
         k1 = [turned_weights(diffs1[half], sq1[:, half]) for half in range(2)]
-        sums(3, whole, True)
+        plain_sums(3)
         open_sums(1)
         for half in range(2):
-            turn_back(half, k1[half], vals1[half], num_ps[1], sum_ps[1])
+            turn_back(1, half, k1[half], vals1[half])
 
         out_rows = out.rearrange("(p t) c -> p t c", t=PACK)
-        inv = ring.tile([P, PACK, S], F32, name="inv", tag="sq_last", bufs=1)
-        for t, cols in [(2, whole), (0, whole), (3, whole), (1, halves[0]), (1, halves[1])]:
-            if (t, cols) == (3, whole):
-                square_sum(1)
-            res = ring.tile([P, cols.stop - cols.start], F32, name="res", bufs=5)
+        inv = ring.tile([P, PACK, S], F32, name="inv", tag="exp_order", bufs=1)
+        pieces = [(2, whole), (0, whole), (3, whole), (1, halves[0]), (1, halves[1])]
+
+        def finish(t, cols):
+            res = ring.tile([P, cols.stop - cols.start], F32, name="res", bufs=len(pieces))
             nc.scalar.activation(inv[:, t, cols], den_sq[:, t, cols], ACT.Abs_reciprocal_sqrt)
             if t < TURNED:
                 nc.vector.scalar_tensor_tensor(res[:], num_ps[t][:, cols], -1.0, inv[:, t, cols], ALU.mult, ALU.mult)
             else:
                 nc.vector.tensor_tensor(res[:], num[:, t - TURNED, cols], inv[:, t, cols], ALU.mult)
             nc.sync.dma_start(out_rows[:, t, cols], res[:])
+
+        for t, cols in pieces[:2]:
+            finish(t, cols)
+        square_sum(1)
+        for t, cols in pieces[2:]:
+            finish(t, cols)

from contextlib import ExitStack

import concourse.mybir as mybir
from concourse.masks import make_identity

K, T, S, N, H = 512, 2048, 512, 512, 512
FLOPS = 2 * S * (K * H + H * N + K * N)

F32 = mybir.dt.float32
BF16 = mybir.dt.bfloat16
I32 = mybir.dt.int32
U32 = mybir.dt.uint32
U16 = mybir.dt.uint16
U8 = mybir.dt.uint8
FP8X4 = mybir.dt.float8_e4m3fn_x4
ACT = mybir.ActivationFunctionType
ALU = mybir.AluOpType

P = 128
PACK = 4
HALF = S // 2
LIST_COLS = S // 16
QUADRANT = 32
VECTOR_CLEARS = 1280
TURNED = 2
H_BANK = (0, 6, 2, 4)
FETCH_DEPTH = 4


def tile_picked_mixhebzkern_none_p_kernel(
    tc, x_words, x_scales, w1, tau, gn, w2, w3, offs, n1, n2, hz, n3, n4, out
):
    nc = tc.nc
    with ExitStack() as ctx:
        lists = ctx.enter_context(tc.tile_pool(name="lists", bufs=1))
        keep = ctx.enter_context(tc.tile_pool(name="keep", bufs=1))
        ring = ctx.enter_context(tc.tile_pool(name="ring", bufs=2))
        psum = ctx.enter_context(tc.psum_pool(name="psum", bufs=1))

        halves = [slice(0, HALF), slice(HALF, S)]
        whole = slice(0, S)

        def load_list(src, name):
            tile = lists.tile([P, LIST_COLS], U16, name=name)
            nc.sync.dma_start(tile[:], src)
            return tile

        def half_of(tile, half):
            return tile[:, half * (LIST_COLS // 2) : (half + 1) * (LIST_COLS // 2)]

        scale_rows = x_scales[0].bitcast(I32)
        xs = keep.tile([P, T], U8, name="xs", align_bytes=64)
        hz_scales = keep.tile([P, S], U8, name="hz_scales", align_bytes=64)
        nc.vector.memset(xs[:, 0:VECTOR_CLEARS].bitcast(I32), 0)
        nc.gpsimd.memset(xs[:, VECTOR_CLEARS:T].bitcast(I32), 0)
        nc.gpsimd.memset(hz_scales[:].bitcast(I32), 0)

        ident = keep.tile([P, P], F32, name="ident")
        make_identity(nc, ident[:])
        half_const = keep.tile([P, 1], F32, name="half_const")
        nc.gpsimd.memset(half_const[:], 0.5)

        offs_t = load_list(offs, "offs_t")
        hz_t = load_list(hz, "hz_t")
        for q in range(4):
            nc.sync.dma_start(
                xs[QUADRANT * q : QUADRANT * q + 4, :].bitcast(I32), scale_rows[4 * q : 4 * q + 4, :]
            )
        nc.sync.dma_start(xs[4:P:8, :].bitcast(I32), scale_rows)
        xw = keep.tile([P, T], I32, name="xw", align_bytes=64)
        nc.sync.dma_start(xw[:], x_words[0].rearrange("p n t -> p (n t)").bitcast(I32))
        w1_rows = w1.rearrange("(p j) c -> p j c", j=PACK)
        w1_raw = []
        for part in range(2):
            raw = keep.tile([P, PACK, H // 2], F32, name=f"w1_raw{part}")
            nc.sync.dma_start(raw[:], w1_rows[:, :, part * (H // 2) : (part + 1) * (H // 2)])
            w1_raw.append(raw)
        tau_t = keep.tile([P, PACK], F32, name="tau_t")
        gn_t = keep.tile([P, PACK], F32, name="gn_t")
        n2_t = load_list(n2, "n2_t")
        n1_t = load_list(n1, "n1_t")
        nc.sync.dma_start(tau_t[:], tau.rearrange("(p t) o -> p (t o)", t=PACK))
        nc.sync.dma_start(gn_t[:], gn.rearrange("(p t) o -> p (t o)", t=PACK))
        w2_raw = keep.tile([P, PACK, N], F32, name="w2_raw")
        w3_raw = keep.tile([P, PACK, N], F32, name="w3_raw")
        nc.sync.dma_start(w2_raw[:], w2.rearrange("(p j) c -> p j c", j=PACK))
        nc.sync.dma_start(w3_raw[:], w3.rearrange("(p j) c -> p j c", j=PACK))
        n3_t = load_list(n3, "n3_t")
        n4_t = load_list(n4, "n4_t")

        pick_scales = keep.tile([P, S], U8, name="pick_scales", align_bytes=64)
        pick_words = keep.tile([P, S], U32, name="pick_words", align_bytes=64)
        hz_bytes = keep.tile([P, S], U8, name="hz_bytes", align_bytes=64)
        nc.vector.tensor_copy(pick_scales[:], xs[:].indirect(offs_t[:]))
        nc.vector.tensor_copy(hz_bytes[:], xs[:].indirect(hz_t[:]))
        nc.vector.tensor_copy(pick_words[:], xw[:].bitcast(U32).indirect(offs_t[:]))
        hz_words = keep.tile([P, S], U32, name="hz_words", align_bytes=64)
        nc.vector.tensor_copy(hz_words[:], xw[:].bitcast(U32).indirect(hz_t[:]))
        neg_tau = keep.tile([P, PACK], F32, name="neg_tau")
        gn_m2 = keep.tile([P, PACK], F32, name="gn_m2")

        def deal(engine_copy, raw, t0, t1, name):
            m = raw.shape[2] // PACK
            dealt = keep.tile([P, t1 - t0, m, PACK], BF16, name=name, align_bytes=64)
            engine_copy(
                dealt[:].rearrange("p t m j -> p m j t"),
                raw[:].rearrange("p j (m t) -> p m j t", t=PACK)[:, :, :, t0:t1],
            )
            return dealt

        w1_codes = keep.tile([P, PACK, P], U32, name="w1_codes", align_bytes=64)
        w1_scales = keep.tile([P, PACK, P], U8, name="w1_scales", align_bytes=64)
        w1_low = deal(nc.scalar.copy, w1_raw[0], 0, 4, "w1_dealt0")
        w1_high = [
            deal(nc.vector.tensor_copy, w1_raw[1], 0, 2, "w1_dealt1"),
            deal(nc.scalar.copy, w1_raw[1], 2, 4, "w1_dealt2"),
        ]
        y_ps = []
        for t in range(PACK):
            for part, dealt in enumerate((w1_low[:, t], w1_high[t // 2][:, t % 2])):
                m_cols = slice(part * (P // 2), (part + 1) * (P // 2))
                nc.vector.quantize_mx(
                    out=w1_codes[:, t, m_cols].bitcast(FP8X4),
                    scales=w1_scales[:, t, m_cols],
                    in_=dealt.rearrange("p m j -> p (m j)"),
                )
            bank = psum.tile([P, S], F32, name=f"y_ps{t}", tag=f"bank{t}")
            nc.tensor.matmul_mx(
                out=bank[:],
                lhsT=w1_codes[:, t, :].bitcast(FP8X4),
                lhsT_scale=w1_scales[:, t, :],
                rhs=pick_words[:].bitcast(FP8X4),
                rhs_scale=pick_scales[:],
                start=True,
                stop=True,
            )
            y_ps.append(bank)

        nc.scalar.activation(neg_tau[:], tau_t[:], ACT.Copy, scale=-1.0)
        nc.scalar.activation(gn_m2[:], gn_t[:], ACT.Copy, scale=-2.0)
        y_sb, lows = [], []
        for t in range(PACK):
            y_t = keep.tile([P, S], F32, name=f"y{t}")
            low = keep.tile([P, 1], F32, name=f"low{t}", align_bytes=64)
            nc.vector.tensor_scalar(y_t[:], y_ps[t][:], 1.0, None, ALU.mult, ALU.min, accum_out=low[:])
            y_sb.append(y_t)
            lows.append(low)

        for j in range(4):
            nc.sync.dma_start(
                hz_scales[j:P:QUADRANT, :].bitcast(I32), hz_bytes[4 + 8 * j : P : QUADRANT, :].bitcast(I32)
            )

        bias = [keep.tile([P, 1], F32, name=f"bias{t}") for t in range(PACK)]
        z = [keep.tile([P, PACK, HALF], F32, name=f"z{half}") for half in range(2)]

        def quantize_pair(dealt, name):
            codes = keep.tile([P, 2, P], U32, name=name + "_codes", align_bytes=64)
            scales = keep.tile([P, 2, P], U8, name=name + "_scales", align_bytes=64)
            nc.vector.quantize_mx(
                out=codes[:].rearrange("p t m -> p (t m)").bitcast(FP8X4),
                scales=scales[:].rearrange("p t m -> p (t m)"),
                in_=dealt[:].rearrange("p t m j -> p (t m j)"),
            )
            return codes, scales

        def fetch_y(t, half):
            y_n2 = ring.tile([P, HALF], F32, name="y_n2", bufs=FETCH_DEPTH)
            ea = ring.tile([P, HALF], F32, name="ea", bufs=FETCH_DEPTH)
            nc.scalar.activation(y_n2[:], y_sb[t][:].indirect(half_of(n2_t, half)), ACT.Copy)
            if half == 0:
                nc.scalar.activation(bias[t][:], lows[t][:], ACT.Copy, scale=tau_t[:, t : t + 1])
            nc.scalar.activation(
                ea[:],
                y_sb[t][:].indirect(half_of(n1_t, half)),
                ACT.Exp,
                bias=bias[t][:],
                scale=neg_tau[:, t : t + 1],
            )
            return y_n2, ea

        def make_z(t, half, y_n2, ea):
            u = ring.tile([P, HALF], F32, name="u", bufs=FETCH_DEPTH)
            nc.vector.scalar_tensor_tensor(u[:], ea[:], gn_m2[:, t : t + 1], y_n2[:], ALU.mult, ALU.mult)
            nc.vector.scalar_tensor_tensor(
                z[half][:, t, :], y_sb[t][:, halves[half]], gn_t[:, t : t + 1], u[:], ALU.mult, ALU.add
            )

        def weave_z(half):
            woven = keep.tile([P, HALF, PACK], BF16, name=f"z_woven{half}", align_bytes=64)
            nc.vector.tensor_copy(
                woven[:].rearrange("p (c i) t -> p c t i", i=4), z[half][:].rearrange("p t (c i) -> p c t i", i=4)
            )
            return woven

        def quantize_z(half, woven):
            codes = keep.tile([P, HALF], U32, name=f"z_codes{half}", align_bytes=64)
            scales = keep.tile([P, HALF], U8, name=f"z_scales{half}", align_bytes=64)
            nc.vector.quantize_mx(
                out=codes[:].bitcast(FP8X4), scales=scales[:], in_=woven[:].rearrange("p c t -> p (c t)")
            )
            return codes, scales

        dealt_pairs, w_mx, z_mx = [], [], []
        pairs = [(w2_raw, 0, "w2a"), (w2_raw, 2, "w2b"), (w3_raw, 0, "w3a"), (w3_raw, 2, "w3b")]
        for t in range(PACK):
            fetched = fetch_y(t, 0)
            raw, t0, name = pairs[t]
            dealt_pairs.append(deal(nc.vector.tensor_copy, raw, t0, t0 + 2, name + "_dealt"))
            if t >= 1:
                w_mx.append(quantize_pair(dealt_pairs[t - 1], pairs[t - 1][2]))
            make_z(t, 0, *fetched)
        for t in range(PACK):
            fetched = fetch_y(t, 1)
            if t == 0:
                woven = weave_z(0)
                w_mx.append(quantize_pair(dealt_pairs[-1], pairs[-1][2]))
                z_mx.append(quantize_z(0, woven))
            make_z(t, 1, *fetched)
        z_mx.append(quantize_z(1, weave_z(1)))
        w2_mx, w3_mx = w_mx[0:2], w_mx[2:4]

        h_order = (2, 0, 1, 3)
        h_sb = [keep.tile([P, S], F32, name=f"h{t}") for t in range(PACK)]
        h_ps = {}
        for half in range(2):
            for t in h_order:
                h_ps[t, half] = psum.tile([P, HALF], F32, name=f"h_ps{t}_{half}", tag=f"bank{H_BANK[t] + half}")
                nc.tensor.matmul_mx(
                    out=h_ps[t, half][:],
                    lhsT=w3_mx[t // 2][0][:, t % 2, :].bitcast(FP8X4),
                    lhsT_scale=w3_mx[t // 2][1][:, t % 2, :],
                    rhs=hz_words[:, halves[half]].bitcast(FP8X4),
                    rhs_scale=hz_scales[:, halves[half]],
                    start=True,
                    stop=False,
                )
        for half in range(2):
            for t in h_order:
                nc.tensor.matmul_mx(
                    out=h_ps[t, half][:],
                    lhsT=w2_mx[t // 2][0][:, t % 2, :].bitcast(FP8X4),
                    lhsT_scale=w2_mx[t // 2][1][:, t % 2, :],
                    rhs=z_mx[half][0][:].bitcast(FP8X4),
                    rhs_scale=z_mx[half][1][:],
                    start=False,
                    stop=True,
                )
        for t in h_order:
            nc.scalar.copy(h_sb[t][:, halves[0]], h_ps[t, 0][:])

        num = keep.tile([P, PACK - TURNED, S], F32, name="num")
        den_sq = keep.tile([P, PACK, S], F32, name="den_sq")
        picked = [keep.tile([P, 2, S], F32, name=f"picked{t}") for t in range(PACK)]
        diff = {t: keep.tile([P, 2, S], F32, name=f"diff{t}") for t in range(TURNED, PACK)}
        kern = {t: keep.tile([P, 2, S], F32, name=f"kern{t}") for t in range(TURNED, PACK)}
        den = {t: keep.tile([P, S], F32, name=f"den{t}") for t in range(TURNED, PACK)}
        num_ps, sum_ps = {}, {}

        def fetch_h(t):
            for half in range(2):
                by_n3 = h_sb[t][:].indirect(half_of(n3_t, half))
                by_n4 = h_sb[t][:].indirect(half_of(n4_t, half))
                if t < TURNED:
                    nc.vector.tensor_scalar(picked[t][:, 0, halves[half]], by_n3, -1.0, 0.0, ALU.mult, ALU.add)
                    nc.scalar.activation(picked[t][:, 1, halves[half]], by_n4, ACT.Copy, scale=-1.0)
                else:
                    nc.vector.tensor_copy(picked[t][:, 0, halves[half]], by_n3)
                    nc.scalar.activation(picked[t][:, 1, halves[half]], by_n4, ACT.Copy, scale=1.0)

        def subtract(t, engine):
            for e in range(2):
                engine.tensor_tensor(diff[t][:, e, :], picked[t][:, e, :], h_sb[t][:], ALU.subtract)

        def plain_sums(t):
            prod = ring.tile([P, 2, S], F32, name="prod")
            nc.vector.scalar_tensor_tensor(den[t][:], kern[t][:, 0, :], 0.5, kern[t][:, 1, :], ALU.add, ALU.add)
            nc.vector.tensor_tensor(prod[:], kern[t][:], picked[t][:], ALU.mult)
            nc.vector.tensor_tensor(den_sq[:, t, :], den[t][:], den[t][:], ALU.mult)
            nc.vector.tensor_tensor(num[:, t - TURNED, :], prod[:, 0, :], prod[:, 1, :], ALU.add)

        def block(half, b):
            return slice(half * HALF + b * P, half * HALF + (b + 1) * P)

        def add_transposed(dst, term0, term1):
            nc.tensor.matmul(dst, term0, ident[:], start=True, stop=False, is_transpose=True)
            nc.tensor.matmul(dst, term1, ident[:], start=False, stop=True, is_transpose=True)

        def turn_diff(t, half):
            diff_ps = psum.tile([P, 2, 2, P], F32, name="diff_ps", tag=f"bank{6 * t + half}")
            for e in range(2):
                for b in range(2):
                    add_transposed(diff_ps[:, e, b, :], h_sb[t][:, block(half, b)], picked[t][:, e, block(half, b)])
            return diff_ps

        def turn_vals(t, half):
            vals_ps = psum.tile([P, 2, 2, P], F32, name="vals_ps", tag=f"bank{2 + half}")
            for e in range(2):
                for b in range(2):
                    nc.tensor.transpose(vals_ps[:, e, b, :], picked[t][:, e, block(half, b)], ident[:])
            return vals_ps

        def turned_weights(diff_ps, sq):
            k_turned = ring.tile([P, 2, 2, P], F32, name="k_turned", bufs=FETCH_DEPTH)
            nc.scalar.activation(sq, diff_ps[:], ACT.Square)
            nc.scalar.activation(k_turned[:], sq, ACT.Exp, scale=-0.5)
            return k_turned

        def open_sums(t):
            num_ps[t] = psum.tile([P, S], F32, name=f"num_ps{t}", tag=f"bank{PACK + t}")
            sum_ps[t] = psum.tile([P, S], F32, name=f"sum_ps{t}", tag=f"bank{t}")

        def turn_back(t, half, k_turned, vals_ps):
            prod_turned = ring.tile([P, 2, 2, P], F32, name="prod_turned", bufs=FETCH_DEPTH)
            nc.vector.tensor_tensor(prod_turned[:], k_turned[:], vals_ps[:], ALU.mult)
            for b in range(2):
                add_transposed(sum_ps[t][:, block(half, b)], k_turned[:, 0, b, :], k_turned[:, 1, b, :])
            for b in range(2):
                add_transposed(num_ps[t][:, block(half, b)], prod_turned[:, 0, b, :], prod_turned[:, 1, b, :])

        def square_sum(t):
            nc.scalar.activation(den_sq[:, t, :], sum_ps[t][:], ACT.Square, bias=half_const[:])

        nc.vector.tensor_copy(h_sb[2][:, halves[1]], h_ps[2, 1][:])
        nc.scalar.copy(h_sb[0][:, halves[1]], h_ps[0, 1][:])
        fetch_h(2)
        subtract(2, nc.gpsimd)
        sq2 = ring.tile([P, 2, S], F32, name="sq2", bufs=1)
        for e in range(2):
            nc.gpsimd.tensor_tensor(sq2[:, e, :], diff[2][:, e, :], diff[2][:, e, :], ALU.mult)
        fetch_h(0)
        for t in (1, 3):
            nc.vector.tensor_copy(h_sb[t][:, halves[1]], h_ps[t, 1][:])
        diffs0 = [turn_diff(0, half) for half in range(2)]
        vals0 = [turn_vals(0, half) for half in range(2)]
        fetch_h(1)
        diffs1 = [turn_diff(1, half) for half in range(2)]
        fetch_h(3)
        for e in range(2):
            for half in range(2):
                nc.vector.tensor_tensor(
                    diff[3][:, e, halves[half]], picked[3][:, e, halves[half]], h_ps[3, half][:], ALU.subtract
                )

        sq3 = ring.tile([P, 2, S], F32, name="sq3", tag="exp_order", bufs=1)
        nc.vector.tensor_tensor(sq3[:], diff[3][:], diff[3][:], ALU.mult)
        sq0 = ring.tile([P, 2, 2, 2, P], F32, name="sq0", bufs=1)
        k0 = [turned_weights(diffs0[half], sq0[:, half]) for half in range(2)]
        nc.scalar.activation(kern[2][:], sq2[:], ACT.Exp, scale=-0.5)
        nc.scalar.activation(kern[3][:], sq3[:], ACT.Exp, scale=-0.5)
        open_sums(0)
        vals1 = []
        for half in range(2):
            turn_back(0, half, k0[half], vals0[half])
            vals1.append(turn_vals(1, half))
        plain_sums(2)
        square_sum(0)
        sq1 = ring.tile([P, 2, 2, 2, P], F32, name="sq1", tag="exp_order", bufs=1)
        k1 = [turned_weights(diffs1[half], sq1[:, half]) for half in range(2)]
        plain_sums(3)
        open_sums(1)
        for half in range(2):
            turn_back(1, half, k1[half], vals1[half])

        out_rows = out.rearrange("(p t) c -> p t c", t=PACK)
        inv = ring.tile([P, PACK, S], F32, name="inv", tag="exp_order", bufs=1)
        pieces = [(2, whole), (0, whole), (3, whole), (1, halves[0]), (1, halves[1])]

        def finish(t, cols):
            res = ring.tile([P, cols.stop - cols.start], F32, name="res", bufs=len(pieces))
            nc.scalar.activation(inv[:, t, cols], den_sq[:, t, cols], ACT.Abs_reciprocal_sqrt)
            if t < TURNED:
                nc.vector.scalar_tensor_tensor(res[:], num_ps[t][:, cols], -1.0, inv[:, t, cols], ALU.mult, ALU.mult)
            else:
                nc.vector.tensor_tensor(res[:], num[:, t - TURNED, cols], inv[:, t, cols], ALU.mult)
            nc.sync.dma_start(out_rows[:, t, cols], res[:])

        for t, cols in pieces[:2]:
            finish(t, cols)
        square_sum(1)
        for t, cols in pieces[2:]:
            finish(t, cols)
